import numpy as np
import ml_dtypes


def mxq(x, axis, fmt="e4m3"):
    dtype, down = {"e4m3": (ml_dtypes.float8_e4m3fn, 7), "e5m2": (ml_dtypes.float8_e5m2, 14)}[fmt]
    v = np.moveaxis(np.asarray(x, np.float32).astype(ml_dtypes.bfloat16).astype(np.float64), axis, -1)
    blocks = v.reshape(v.shape[:-1] + (-1, 32))
    amax = np.abs(blocks).max(-1, keepdims=True)
    byte = np.maximum(np.where(amax > 0, np.frexp(amax)[1] - 1 + 127, 0) - down, 1)
    scale = np.exp2(byte - 127.0)
    codes = (blocks / scale).astype(np.float32).astype(dtype).astype(np.float64)
    return np.moveaxis((codes * scale).reshape(v.shape), -1, axis)


WIDE = False


def mx_kscale(k):
    if not WIDE:
        return np.ones(k)
    levels = np.array([10, -10, 5, -5, 0])
    if k % 512:
        return np.exp2(np.random.permutation(np.resize(levels, k // 32))).repeat(32)
    a = np.empty((k // 512, 16))
    for p in range(k // 512):
        a[p, :8] = np.random.permutation(np.resize(levels, 8))
        for g in range(8):
            far = levels[np.abs(levels - a[p, g]) >= 10]
            a[p, g + 8] = far[np.random.randint(len(far))]
    return np.exp2(a.ravel()).repeat(32)


BF16 = ml_dtypes.bfloat16


def bf(x):
    return np.asarray(x, np.float32).astype(BF16)


def f64(x):
    return np.asarray(x).astype(np.float64)


B, C, G, J = 1024, 1536, 3, 512

SHARE = 0.35


def setup_inputs():
    s = mx_kscale(C)
    u = mx_kscale(B)
    v = mx_kscale(C)
    return {"student": bf(np.random.standard_normal((B, C)) * u[:, None] * v),
            "teacher": bf(np.random.standard_normal((B, C)) * u[:, None] * s),
            "confusion": bf(SHARE * np.random.standard_normal((C, C)) / np.sqrt(C) / s[:, None] * v),
            "affinity": bf(SHARE * np.random.standard_normal((B, B)) / np.sqrt(B) / u),
            "keep": bf((1 + 0.1 * np.random.standard_normal(B)) / u),
            "within": bf(SHARE * np.random.standard_normal((C, J)) / np.sqrt(J) / v[:, None]),
            "gain": bf((1 + 0.1 * np.random.standard_normal(C)) / v)}


def reference(student, teacher, confusion, affinity, keep, within, gain):
    d1 = mxq(f64(teacher), 1, "e4m3") @ mxq(f64(confusion), 0, "e4m3")
    z1 = f64(student) + d1
    d2 = mxq(f64(affinity), 1, "e4m3") @ mxq(z1, 0, "e4m3")
    z2 = f64(keep)[:, None] * z1 + d2
    zq = mxq(z2, 1, "e4m3").reshape(B, G, J).swapaxes(0, 1)
    wq = mxq(f64(within), 0, "e4m3").reshape(G, J, J)
    d3 = zq @ wq
    return f64(gain) * z2 + d3.swapaxes(0, 1).reshape(B, C)

from contextlib import ExitStack

import concourse.mybir as mybir
from concourse.masks import make_identity

B, C, G, J = 1024, 1536, 3, 512
P = 128
K_PASS = 512
FLOPS = 2 * B * C * C + 2 * B * B * C + 2 * B * C * J

F32 = mybir.dt.float32
BF16 = mybir.dt.bfloat16
U32 = mybir.dt.uint32
U8 = mybir.dt.uint8
FP8X4 = mybir.dt.float8_e4m3fn_x4
MULT = mybir.AluOpType.mult
ADD = mybir.AluOpType.add

LEAD = 1


def tile_teacher_student_logits_t1_kernel(
    tc, student, teacher, confusion, affinity, keep, within, gain, out
):
    nc = tc.nc
    with ExitStack() as ctx:
        raw = ctx.enter_context(tc.tile_pool(name="raw", bufs=13))
        trow = ctx.enter_context(tc.tile_pool(name="trow", bufs=4))
        const = ctx.enter_context(tc.tile_pool(name="const", bufs=1))
        grp = ctx.enter_context(tc.tile_pool(name="grp", bufs=5))
        zgrp = ctx.enter_context(tc.tile_pool(name="zgrp", bufs=2))
        z2grp = ctx.enter_context(tc.tile_pool(name="z2grp", bufs=4))
        z1pool = ctx.enter_context(tc.tile_pool(name="z1pool", bufs=4))
        z2pool = ctx.enter_context(tc.tile_pool(name="z2pool", bufs=6))
        gzpool = ctx.enter_context(tc.tile_pool(name="gzpool", bufs=6))
        outpool = ctx.enter_context(tc.tile_pool(name="outpool", bufs=3))
        cpool = ctx.enter_context(tc.tile_pool(name="cpool", bufs=2))
        z2codes = ctx.enter_context(tc.tile_pool(name="z2codes", bufs=6))
        keepc = ctx.enter_context(tc.tile_pool(name="keepc", bufs=1))
        psum = ctx.enter_context(tc.psum_pool(name="psum", bufs=8))

        teacher_v = teacher.rearrange("(g p t) k -> g p t k", p=P, t=4)
        affinity_v = affinity.rearrange("(g p t) k -> g p t k", p=P, t=4)
        student_v = student.rearrange("(g p t) c -> g p t c", p=P, t=4)
        confusion_v = confusion.rearrange("(c p j) n -> c p j n", p=P, j=4)
        within_v = within.rearrange("(h p j) n -> h p j n", p=P, j=4)
        out_v = out.rearrange("(g p t) c -> g p t c", p=P, t=4)

        ident = const.tile([P, P], F32, name="ident", tag="ident")
        make_identity(nc, ident[:])
        keep16 = const.tile([P, 2, 4], BF16, name="keep16", tag="keep16")
        keep32 = const.tile([P, 2, 4], F32, name="keep32", tag="keep32")
        gain_sb = const.tile([P, C], BF16, name="gain_sb", tag="gain_sb")

        conf_raw = {}
        stu_raw = {}
        tea_raw = {}
        aff_raw = {}
        win_raw = {}

        def raw_tile():
            return raw.tile([P, 4, 512], BF16, name="rawt", tag="rawt", align_bytes=64)

        def load_conf(h, c):
            t = raw_tile()
            nc.sync.dma_start(out=t[:], in_=confusion_v[c, :, :, h * 512 : (h + 1) * 512])
            conf_raw[h, c] = t

        def load_student(h, g):
            t = raw_tile()
            nc.sync.dma_start(out=t[:], in_=student_v[g, :, :, h * 512 : (h + 1) * 512])
            stu_raw[h, g] = t

        def load_teacher(g, q):
            t = trow.tile([P, 2, C], BF16, name="teat", tag="teat", align_bytes=64)
            nc.sync.dma_start(out=t[:], in_=teacher_v[g, :, 2 * q : 2 * q + 2, :])
            tea_raw[g, q] = t

        def load_affinity(g, q):
            t = raw.tile([P, 2, B], BF16, name="rawt", tag="rawt", align_bytes=64)
            nc.sync.dma_start(out=t[:], in_=affinity_v[g, :, 2 * q : 2 * q + 2, :])
            aff_raw[g, q] = t

        def load_within(h):
            t = raw_tile()
            nc.sync.dma_start(out=t[:], in_=within_v[h])
            win_raw[h] = t

        load_teacher(0, 0)
        load_teacher(0, 1)
        for c in range(3):
            load_conf(0, c)
        load_teacher(1, 0)
        load_student(0, 0)
        load_teacher(1, 1)
        load_affinity(0, 0)
        load_affinity(0, 1)
        load_student(0, 1)
        nc.sync.dma_start(out=keep16[:], in_=keep.rearrange("(g p t) -> p g t", p=P, t=4))
        load_affinity(1, 0)
        load_affinity(1, 1)
        for c in range(3):
            load_conf(1, c)
        load_student(1, 0)
        nc.sync.dma_start(out=gain_sb[:], in_=gain.partition_broadcast(P))
        load_within(0)
        load_student(1, 1)
        for c in range(3):
            load_conf(2, c)
        load_student(2, 0)
        load_within(1)
        load_student(2, 1)
        load_within(2)

        conf_codes = {}
        conf_scales = {}
        tea_codes = {}
        tea_scales = {}
        aff_codes = {}
        aff_scales = {}
        win_codes = {}
        win_scales = {}
        z1_codes = {}
        z1_scales = {}
        z1_f32 = {}
        z1_grp = {}
        grouped_t = {}

        def interleave(engine, key, src, parts=((0, 512),)):
            if key not in grouped_t:
                grouped_t[key] = grp.tile([P, 512, 4], BF16, name="grouped", tag="grouped", align_bytes=64)
            dst = grouped_t[key]
            for lo, hi in parts:
                o = dst[:, lo:hi, :].rearrange("p (n i) t -> p n t i", i=4)
                s = src[:, :, lo:hi].rearrange("p t (n i) -> p n t i", i=4)
                if engine == "v":
                    nc.vector.tensor_copy(out=o, in_=s)
                elif engine == "s":
                    nc.scalar.copy(out=o, in_=s)
                else:
                    nc.gpsimd.tensor_scalar(out=o, in0=s, scalar1=1.0, scalar2=0.0, op0=MULT, op1=ADD)

        def quant_conf(h, c):
            if h not in conf_codes:
                conf_codes[h] = cpool.tile([P, 3, 512], U32, name="ccodes", tag="ccodes", align_bytes=64)
                conf_scales[h] = cpool.tile([P, 3, 512], U8, name="cscales", tag="cscales", align_bytes=64)
            nc.vector.quantize_mx(
                out=conf_codes[h][:, c, :].bitcast(FP8X4),
                scales=conf_scales[h][:, c, :],
                in_=grouped_t["c", h, c][:].rearrange("p n t -> p (n t)"),
            )

        def quant_within(h):
            win_codes[h] = cpool.tile([P, 512], U32, name="wcodes", tag="wcodes", align_bytes=64)
            win_scales[h] = cpool.tile([P, 512], U8, name="wscales", tag="wscales", align_bytes=64)
            nc.vector.quantize_mx(
                out=win_codes[h][:].bitcast(FP8X4),
                scales=win_scales[h][:],
                in_=grouped_t["w", h][:].rearrange("p n t -> p (n t)"),
            )

        banks = {}

        def turn(kind, g, q, c):
            src = (tea_raw if kind == "t" else aff_raw)[g, q]
            words = src[:].bitcast(F32)
            bank = psum.tile([P, 2, 2, P], F32, name="bank", tag="bank")
            for a in range(2):
                for u in range(2):
                    nc.tensor.transpose(bank[:, a, u, :], words[:, a, 256 * c + u : 256 * (c + 1) : 2], ident[:])
            banks[kind, g, q, c] = bank

        def turn_copy(kind, g, q, c):
            dst = grp.tile([P, 256, 4], BF16, name="grouped", tag="grouped", align_bytes=64)
            nc.scalar.copy(
                out=dst[:].bitcast(F32).rearrange("p (a r) u -> p a r u", a=2),
                in_=banks[kind, g, q, c][:].rearrange("p a u r -> p a r u"),
            )
            grouped_t[kind, g, q, c] = dst

        def turn_quant(kind, g, q, c):
            codes, scales, n = (tea_codes, tea_scales, 3) if kind == "t" else (aff_codes, aff_scales, 2)
            if (g, q) not in codes:
                codes[g, q] = keepc.tile([P, n, 256], U32, name=f"{kind}codes{g}{q}", tag=f"{kind}codes{g}{q}", align_bytes=64)
                scales[g, q] = keepc.tile([P, n, 256], U8, name=f"{kind}scales{g}{q}", tag=f"{kind}scales{g}{q}", align_bytes=64)
            nc.vector.quantize_mx(
                out=codes[g, q][:, c, :].bitcast(FP8X4),
                scales=scales[g, q][:, c, :],
                in_=grouped_t[kind, g, q, c][:].rearrange("p n t -> p (n t)"),
            )

        def mm1(k, passes=(0, 1, 2)):
            h, g, q = k // 4, k // 2 % 2, k % 2
            for a in range(2):
                if passes[0] == 0:
                    banks["s1", k, a] = psum.tile([P, 512], F32, name="bank", tag="bank")
            if len(passes) == 3:
                order = [(a, c) for a in range(2) for c in passes]
            else:
                order = [(a, c) for c in passes for a in range(2)]
            for a, c in order:
                cols = slice(a * P, (a + 1) * P)
                nc.tensor.matmul_mx(
                    out=banks["s1", k, a][:],
                    lhsT=tea_codes[g, q][:, c, cols].bitcast(FP8X4),
                    lhsT_scale=tea_scales[g, q][:, c, cols],
                    rhs=conf_codes[h][:, c, :].bitcast(FP8X4),
                    rhs_scale=conf_scales[h][:, c, :],
                    start=(c == 0),
                    stop=(c == 2),
                )

        def add1(k):
            h, g, q = k // 4, k // 2 % 2, k % 2
            if (h, g) not in z1_f32:
                z1_f32[h, g] = z1pool.tile([P, 4, 512], F32, name="z1", tag="z1", align_bytes=64)
            for a in range(2):
                t = 2 * q + a
                nc.vector.tensor_tensor(
                    out=z1_f32[h, g][:, t, :].rearrange("p (u m) -> p u m", u=4),
                    in0=banks["s1", k, a][:].rearrange("p (m u) -> p u m", u=4),
                    in1=stu_raw[h, g][:, t, :].rearrange("p (m u) -> p u m", u=4),
                    op=ADD,
                )

        def z1_round(h, g, half):
            if half == 0:
                z1_grp[h, g] = zgrp.tile([P, 512, 4], BF16, name="zgrouped", tag="zgrouped", align_bytes=64)
            cols = slice(half * 256, half * 256 + 256)
            nc.scalar.copy(
                out=z1_grp[h, g][:, cols, :].rearrange("p (n i) t -> p n t i", i=4),
                in_=z1_f32[h, g][:, :, cols].rearrange("p t (n i) -> p n t i", i=4),
            )

        def z1_quant(h, g, half):
            if half == 0:
                z1_codes[h, g] = cpool.tile([P, 512], U32, name=f"zcodes{g}", tag=f"zcodes{g}", align_bytes=64)
                z1_scales[h, g] = cpool.tile([P, 512], U8, name=f"zscales{g}", tag=f"zscales{g}", align_bytes=64)
            cols = slice(half * 256, half * 256 + 256)
            nc.vector.quantize_mx(
                out=z1_codes[h, g][:, cols].bitcast(FP8X4),
                scales=z1_scales[h, g][:, cols],
                in_=z1_grp[h, g][:, cols, :].rearrange("p n t -> p (n t)"),
            )

        z2_f32 = {}
        gz_f32 = {}
        z2_grp = {}
        z2_codes = {}
        z2_scales = {}
        outs = {}

        def mm2(s):
            h, g, q = s // 4, s // 2 % 2, s % 2
            for a in range(2):
                bank = psum.tile([P, 512], F32, name="bank", tag="bank")
                banks["s2", s, a] = bank
                cols = slice(a * P, (a + 1) * P)
                for c in range(2):
                    nc.tensor.matmul_mx(
                        out=bank[:],
                        lhsT=aff_codes[g, q][:, c, cols].bitcast(FP8X4),
                        lhsT_scale=aff_scales[g, q][:, c, cols],
                        rhs=z1_codes[h, c][:].bitcast(FP8X4),
                        rhs_scale=z1_scales[h, c][:],
                        start=(c == 0),
                        stop=(c == 1),
                    )

        def add2(s):
            h, g, q = s // 4, s // 2 % 2, s % 2
            for a in range(2):
                t = 2 * q + a
                z2 = z2pool.tile([P, 512], F32, name="z2", tag="z2", align_bytes=64)
                nc.vector.scalar_tensor_tensor(
                    out=z2[:],
                    in0=z1_f32[h, g][:, t, :],
                    scalar=keep32[:, g, t : t + 1],
                    in1=banks["s2", s, a][:],
                    op0=MULT,
                    op1=ADD,
                )
                z2_f32[s, a] = z2

        def gain_mul(s):
            h = s // 4
            for a in range(2):
                gz = gzpool.tile([P, 512], F32, name="gz", tag="gz", align_bytes=64)
                nc.gpsimd.tensor_tensor(
                    out=gz[:].rearrange("p (m u) -> p m u", u=4),
                    in0=z2_f32[s, a][:].rearrange("p (u m) -> p m u", u=4),
                    in1=gain_sb[:, h * 512 : (h + 1) * 512].rearrange("p (m u) -> p m u", u=4),
                    op=MULT,
                )
                gz_f32[s, a] = gz

        def turn2(s):
            for a in range(2):
                bank = psum.tile([P, 4, P], F32, name="bank", tag="bank")
                banks["t2", s, a] = bank
                for u in range(4):
                    nc.tensor.transpose(bank[:, u, :], z2_f32[s, a][:, u * P : (u + 1) * P], ident[:])

        def round2(s):
            for a in range(2):
                dst = z2grp.tile([P, P, 4], BF16, name="z2g", tag="z2g", align_bytes=64)
                nc.scalar.copy(out=dst[:], in_=banks["t2", s, a][:].rearrange("p u n -> p n u"))
                z2_grp[s, a] = dst

        def quant2(s):
            for a in range(2):
                codes = z2codes.tile([P, P], U32, name="z2c", tag="z2c", align_bytes=64)
                scales = z2codes.tile([P, P], U8, name="z2s", tag="z2s", align_bytes=64)
                nc.vector.quantize_mx(
                    out=codes[:].bitcast(FP8X4),
                    scales=scales[:],
                    in_=z2_grp[s, a][:].rearrange("p n t -> p (n t)"),
                )
                z2_codes[s, a] = codes
                z2_scales[s, a] = scales

        def mm3(s):
            h = s // 4
            for a in range(2):
                bank = psum.tile([P, 512], F32, name="bank", tag="bank")
                banks["s3", s, a] = bank
                nc.tensor.matmul_mx(
                    out=bank[:],
                    lhsT=z2_codes[s, a][:].bitcast(FP8X4),
                    lhsT_scale=z2_scales[s, a][:],
                    rhs=win_codes[h][:].bitcast(FP8X4),
                    rhs_scale=win_scales[h][:],
                    start=True,
                    stop=True,
                )

        def add3(s):
            outs[s] = outpool.tile([P, 2, 512], F32, name="outt", tag="outt", align_bytes=64)
            for a in range(2):
                nc.vector.tensor_tensor(out=outs[s][:, a, :], in0=banks["s3", s, a][:], in1=gz_f32[s, a][:], op=ADD)

        def store(s):
            h, g, q = s // 4, s // 2 % 2, s % 2
            nc.sync.dma_start(out=out_v[g, :, 2 * q : 2 * q + 2, h * 512 : (h + 1) * 512], in_=outs[s][:])

        HB = ((0, 256), (256, 512))
        HA = ((0, 256),)
        HC = ((256, 512),)

        def turns(kind, g, q):
            for c in range(3 if kind == "t" else 2):
                turn(kind, g, q, c)
                turn_copy(kind, g, q, c)

        def turn_quants(kind, g, q):
            for c in range(3 if kind == "t" else 2):
                turn_quant(kind, g, q, c)

        turns("t", 0, 0)
        turn_quants("t", 0, 0)
        turns("t", 0, 1)
        interleave("v", ("c", 0, 0), conf_raw[0, 0])
        turn_quants("t", 0, 1)
        quant_conf(0, 0)
        mm1(0, (0,))
        mm1(1, (0,))
        interleave("v", ("c", 0, 1), conf_raw[0, 1], HA)
        interleave("s", ("c", 0, 1), conf_raw[0, 1], HC)
        interleave("v", ("c", 0, 2), conf_raw[0, 2], HA)
        interleave("s", ("c", 0, 2), conf_raw[0, 2], HC)
        quant_conf(0, 1)
        mm1(0, (1,))
        mm1(1, (1,))
        quant_conf(0, 2)
        turns("t", 1, 0)
        mm1(0, (2,))
        mm1(1, (2,))
        turn_quants("t", 1, 0)
        add1(0)
        turns("t", 1, 1)
        add1(1)
        mm1(2)
        turn_quants("t", 1, 1)
        z1_round(0, 0, 0)
        z1_round(0, 0, 1)
        mm1(3)
        add1(2)
        z1_quant(0, 0, 0)
        z1_quant(0, 0, 1)
        turns("a", 0, 0)
        turns("a", 0, 1)
        turns("a", 1, 0)
        add1(3)
        z1_round(0, 1, 0)
        z1_round(0, 1, 1)
        turns("a", 1, 1)
        turn_quants("a", 0, 0)
        turn_quants("a", 0, 1)
        nc.vector.tensor_copy(out=keep32[:], in_=keep16[:])
        turn_quants("a", 1, 0)
        z1_quant(0, 1, 0)
        z1_quant(0, 1, 1)
        interleave("v", ("c", 1, 0), conf_raw[1, 0])
        interleave("s", ("c", 1, 1), conf_raw[1, 1], HB)
        turn_quants("a", 1, 1)
        quant_conf(1, 0)

        s1_at = {0: [4], 1: [5], 2: [6, 7], 4: [8], 5: [9], 6: [10, 11]}
        pre_s = {2: [("z1", 1, 0)], 3: [("z1", 1, 1)], 6: [("z1", 2, 0)], 7: [("z1", 2, 1)]}
        side_s = {
            0: [("c", 1, 2)],
            1: [("w", 0), ("c", 2, 0)],
            2: [("c", 2, 1)],
            3: [("c", 2, 2)],
            5: [("w", 1)],
            7: [("w", 2)],
        }
        for s in range(14):
            if s == 0:
                interleave("s", ("c", 1, 2), conf_raw[1, 2], HC)
                interleave("v", ("c", 1, 2), conf_raw[1, 2], HA)
                quant_conf(1, 1)
                quant_conf(1, 2)
            ks = s1_at.get(s, [])
            for item in pre_s.get(s, ()):
                for half in range(2):
                    z1_round(item[1], item[2], half)
            if s < 12:
                mm2(s)
            if 1 <= s < 13:
                turn2(s - 1)
            if s >= 2:
                mm3(s - 2)
            for k in ks:
                mm1(k)
            if s < 12:
                add2(s)
                gain_mul(s)
            if 1 <= s < 13:
                round2(s - 1)
            if s >= 2:
                add3(s - 2)
                store(s - 2)
            for k in ks:
                add1(k)
            for item in pre_s.get(s, ()):
                for half in range(2):
                    z1_quant(item[1], item[2], half)
            if s > 0:
                for item in side_s.get(s, ()):
                    if item[0] == "c":
                        interleave("s", item, conf_raw[item[1], item[2]], HB)
                    else:
                        interleave("s", item, win_raw[item[1]], HB)
            if 1 <= s < 13:
                quant2(s - 1)
            if s > 0:
                for item in side_s.get(s, ()):
                    if item[0] == "c":
                        quant_conf(item[1], item[2])
                    else:
                        quant_within(item[1])
